import numpy as np
import ml_dtypes


def mxq(x, axis, fmt="e4m3"):
    dtype, down = {"e4m3": (ml_dtypes.float8_e4m3fn, 7), "e5m2": (ml_dtypes.float8_e5m2, 14)}[fmt]
    v = np.moveaxis(np.asarray(x, np.float32).astype(ml_dtypes.bfloat16).astype(np.float64), axis, -1)
    blocks = v.reshape(v.shape[:-1] + (-1, 32))
    amax = np.abs(blocks).max(-1, keepdims=True)
    byte = np.maximum(np.where(amax > 0, np.frexp(amax)[1] - 1 + 127, 0) - down, 1)
    scale = np.exp2(byte - 127.0)
    codes = (blocks / scale).astype(np.float32).astype(dtype).astype(np.float64)
    return np.moveaxis((codes * scale).reshape(v.shape), -1, axis)


WIDE = False


def mx_kscale(k):
    if not WIDE:
        return np.ones(k)
    levels = np.array([10, -10, 5, -5, 0])
    if k % 512:
        return np.exp2(np.random.permutation(np.resize(levels, k // 32))).repeat(32)
    a = np.empty((k // 512, 16))
    for p in range(k // 512):
        a[p, :8] = np.random.permutation(np.resize(levels, 8))
        for g in range(8):
            far = levels[np.abs(levels - a[p, g]) >= 10]
            a[p, g + 8] = far[np.random.randint(len(far))]
    return np.exp2(a.ravel()).repeat(32)


def f64(x):
    return np.asarray(x).astype(np.float64)


def striped8(idx):
    return np.asarray(idx).reshape(8, -1, 16).transpose(0, 2, 1).reshape(128, -1).astype(np.uint16)


def unstriped8(offs):
    return offs.reshape(8, 16, -1).transpose(0, 2, 1).reshape(8, -1).astype(np.int64)


def pick8(x, idx, run):
    r = np.arange(len(x))
    return x[r[:, None], idx[r % (8 * run) // run]]


E2M1 = np.array([0.0, 0.5, 1.0, 1.5, 2.0, 3.0, 4.0, 6.0, -0.0, -0.5, -1.0, -1.5, -2.0, -3.0, -4.0, -6.0])


def pack_weight(w, fmt):
    k, n = w.shape
    w = f64(np.asarray(w, np.float32).astype(ml_dtypes.bfloat16)).reshape(k // 32, 32, n)
    amax = np.abs(w).max(1)
    if fmt == "e4m3":
        byte = np.frexp(amax)[1] - 1 + 127 - 7
    else:
        mant, ex = np.frexp(amax / 6.0)
        byte = np.where(mant > 0.5, ex, ex - 1) + 127
    byte = np.clip(np.where(amax > 0, byte, 1), 1, 254)
    scaled = (w * np.exp2(127.0 - byte)[:, None, :]).reshape(k, n).astype(np.float32)
    by_word = np.ascontiguousarray(scaled.reshape(k // 512, 128, 4, n).transpose(0, 1, 3, 2))
    if fmt == "e4m3":
        words = by_word.astype(ml_dtypes.float8_e4m3fn).view(np.uint8)
    else:
        c = by_word.astype(ml_dtypes.float4_e2m1fn).view(np.uint8) & 0xF
        words = (c[..., 0::2] | (c[..., 1::2] << 4)).reshape(k // 512, 128, 2 * n)
    return np.ascontiguousarray(words), np.ascontiguousarray(byte.astype(np.uint8).reshape(k // 512, 16, n))


def unpack_weight(words, scales, fmt):
    g, _, n = scales.shape
    words = np.ascontiguousarray(words).reshape(g, 128, n, -1)
    if fmt == "e4m3":
        vals = words.view(ml_dtypes.float8_e4m3fn).astype(np.float64)
    else:
        nib = np.empty((g, 128, n, 4), np.uint8)
        nib[..., 0::2] = words & 0xF
        nib[..., 1::2] = words >> 4
        vals = E2M1[nib]
    vals = vals * np.repeat(np.exp2(scales.astype(np.float64) - 127.0), 8, axis=1)[..., None]
    return vals.transpose(0, 1, 3, 2).reshape(g * 512, n)


D, T, U, X, S, I, Q = 512, 1024, 1024, 1024, 1024, 512, 128


def setup_inputs():
    n = np.random.standard_normal
    idx = np.stack([np.random.permutation(T)[:I] for _ in range(8)])
    idx2 = np.stack([np.random.permutation(U)[:I] for _ in range(8)])
    idx3 = np.stack([np.random.permutation(U)[:I] for _ in range(8)])
    idx4 = np.stack([np.random.permutation(X)[:I] for _ in range(8)])
    idx5 = np.stack([np.random.permutation(X)[:I] for _ in range(8)])
    idx6 = np.stack([np.random.permutation(S)[:I] for _ in range(8)])
    idx7 = np.stack([np.random.permutation(S)[:I] for _ in range(8)])
    fd = mx_kscale(D)
    keysp = pack_weight(n((D, T)) / fd[:, None], "e2m1")
    notesp = pack_weight(n((D, U)) / fd[:, None], "e4m3")
    usersp = pack_weight(n((D, X)) / fd[:, None], "e2m1")
    shelvesp = pack_weight(n((D, S)) / fd[:, None], "e4m3")
    return {
        "query": (n((D, Q)) * 1.0 / np.sqrt(D) * fd[:, None]).astype(np.float32),
        "keys_words": keysp[0],
        "keys_scales": keysp[1],
        "notes_words": notesp[0],
        "notes_scales": notesp[1],
        "users_words": usersp[0],
        "users_scales": usersp[1],
        "shelves_words": shelvesp[0],
        "shelves_scales": shelvesp[1],
        "offs": striped8(idx),
        "offs2": striped8(idx2),
        "offs3": striped8(idx3),
        "offs4": striped8(idx4),
        "offs5": striped8(idx5),
        "offs6": striped8(idx6),
        "offs7": striped8(idx7),
    }


def reference(query, keys_words, keys_scales, notes_words, notes_scales, users_words, users_scales, shelves_words, shelves_scales, offs, offs2, offs3, offs4, offs5, offs6, offs7):
    idx = unstriped8(offs)
    idx2 = unstriped8(offs2)
    idx3 = unstriped8(offs3)
    idx4 = unstriped8(offs4)
    idx5 = unstriped8(offs5)
    idx6 = unstriped8(offs6)
    idx7 = unstriped8(offs7)
    keysu = unpack_weight(keys_words, keys_scales, "e2m1")
    notesu = unpack_weight(notes_words, notes_scales, "e4m3")
    usersu = unpack_weight(users_words, users_scales, "e2m1")
    shelvesu = unpack_weight(shelves_words, shelves_scales, "e4m3")
    queryq = mxq(f64(query), 0, "e4m3")
    a = queryq.T @ keysu
    b = queryq.T @ notesu
    c0 = queryq.T @ usersu
    d0 = queryq.T @ shelvesu
    f1 = np.zeros((Q, U))
    f1[np.arange(Q)[:, None], idx2[np.arange(Q) % 128 // 16]] = pick8(a, idx, 16)
    bb = b + f1
    f2 = np.zeros((Q, X))
    f2[np.arange(Q)[:, None], idx4[np.arange(Q) % 128 // 16]] = pick8(bb, idx3, 16)
    cc = c0 - f2
    f3 = np.zeros((Q, S))
    f3[np.arange(Q)[:, None], idx6[np.arange(Q) % 128 // 16]] = pick8(cc, idx5, 16)
    dd = d0 + f3
    y = pick8(dd, idx7, 16)
    return y

@@ -1,0 +1,131 @@
+from contextlib import ExitStack
+
+import concourse.mybir as mybir
+
+D, POOL, SLOTS, Q = 512, 1024, 512, 128
+FLOPS = 4 * 2 * D * POOL * Q
+
+F32 = mybir.dt.float32
+BF16 = mybir.dt.bfloat16
+I32 = mybir.dt.int32
+U32 = mybir.dt.uint32
+U16 = mybir.dt.uint16
+U8 = mybir.dt.uint8
+FP8X4 = mybir.dt.float8_e4m3fn_x4
+FP4X4 = mybir.dt.float4_e2m1fn_x4
+ADD = mybir.AluOpType.add
+SUB = mybir.AluOpType.subtract
+COPY = mybir.ActivationFunctionType.Copy
+
+P = 128
+PACK = 4
+BANK = 512
+HALF = SLOTS // 2
+LIST_COLS = SLOTS // 16
+
+
+def tile_attend_relayfour_four_kernel(
+    tc, query, keys_words, keys_scales, notes_words, notes_scales, users_words, users_scales,
+    shelves_words, shelves_scales, offs, offs2, offs3, offs4, offs5, offs6, offs7, out,
+):
+    nc = tc.nc
+    with ExitStack() as ctx:
+        held = ctx.enter_context(tc.tile_pool(name="held", bufs=1))
+        psum = ctx.enter_context(tc.psum_pool(name="psum", bufs=1))
+
+        def load_list(source, name):
+            tile = held.tile([P, LIST_COLS], U16, name=name)
+            nc.sync.dma_start(tile[:], source)
+            return tile
+
+        def load_scales(source, name, queue):
+            plane = held.tile([P, POOL], U8, name=name, align_bytes=64)
+            rows = source[0].bitcast(I32)
+            for quad in range(4):
+                queue.dma_start(plane[32 * quad : 32 * quad + 4, :].bitcast(I32), rows[4 * quad : 4 * quad + 4, :])
+            return plane
+
+        def load_words(source, name, width):
+            words = held.tile([P, POOL * width], U8, name=name, align_bytes=64)
+            nc.sync.dma_start(words[:].bitcast(I32), source.bitcast(I32))
+            return words
+
+        q_raw = held.tile([P, PACK, Q], F32, name="q_raw")
+        nc.sync.dma_start(q_raw[:], query.rearrange("(p j) q -> p j q", j=PACK))
+        keys_plane = load_scales(keys_scales, "keys_plane", nc.scalar)
+        keys = load_words(keys_words[0], "keys", 2)
+        list1 = load_list(offs, "list1")
+        list2 = load_list(offs2, "list2")
+        notes_plane = load_scales(notes_scales, "notes_plane", nc.sync)
+        notes = load_words(notes_words[0].rearrange("p n t -> p (n t)"), "notes", 4)
+        list3 = load_list(offs3, "list3")
+        list4 = load_list(offs4, "list4")
+        users_plane = load_scales(users_scales, "users_plane", nc.sync)
+        users = load_words(users_words[0], "users", 2)
+        list5 = load_list(offs5, "list5")
+        list6 = load_list(offs6, "list6")
+        shelves_plane = load_scales(shelves_scales, "shelves_plane", nc.sync)
+        shelves = load_words(shelves_words[0].rearrange("p n t -> p (n t)"), "shelves", 4)
+        list7 = load_list(offs7, "list7")
+
+        placed = [held.tile([P, POOL], F32, name="placed%d" % s) for s in range(3)]
+        for tile in placed:
+            nc.vector.memset(tile[:], 0.0)
+
+        q_bf = held.tile([P, Q, PACK], BF16, name="q_bf", align_bytes=64)
+        nc.vector.tensor_copy(q_bf[:], q_raw[:].rearrange("p j q -> p q j"))
+        q_codes = held.tile([P, Q], U32, name="q_codes", align_bytes=64)
+        q_plane = held.tile([P, Q], U8, name="q_plane", align_bytes=64)
+        nc.vector.quantize_mx(
+            out=q_codes[:].bitcast(FP8X4), scales=q_plane[:], in_=q_bf[:].rearrange("p q j -> p (q j)")
+        )
+
+        def score(words, plane, width, dtype, first_bank, cols):
+            banks = []
+            for piece in range(POOL // cols):
+                bank = psum.tile([P, cols], F32, name="bank%d" % (first_bank + piece))
+                lo, hi = piece * cols, (piece + 1) * cols
+                nc.tensor.matmul_mx(
+                    bank[:],
+                    lhsT=q_codes[:].bitcast(FP8X4),
+                    lhsT_scale=q_plane[:],
+                    rhs=words[:, lo * width : hi * width].bitcast(dtype),
+                    rhs_scale=plane[:, lo:hi],
+                    start=True,
+                    stop=True,
+                )
+                banks.append(bank)
+            return banks
+
+        def look_up(table, offsets, name):
+            picked = held.tile([P, SLOTS], F32, name=name)
+            nc.vector.tensor_copy(picked[:, :HALF], table[:].indirect(offsets[:, : LIST_COLS // 2]))
+            nc.scalar.activation(picked[:, HALF:], table[:].indirect(offsets[:, LIST_COLS // 2 :]), COPY)
+            return picked
+
+        A_COLS = 256
+        a_banks = score(keys, keys_plane, 2, FP4X4, 0, A_COLS)
+        table = held.tile([P, POOL], F32, name="a")
+        for piece, bank in enumerate(a_banks):
+            cols = table[:, piece * A_COLS : (piece + 1) * A_COLS]
+            if piece % 2 == 0:
+                nc.scalar.activation(cols, bank[:], COPY)
+            else:
+                nc.vector.tensor_copy(cols, bank[:])
+
+        stages = [
+            (score(notes, notes_plane, 4, FP8X4, 4, BANK), list1, list2, ADD),
+            (score(users, users_plane, 2, FP4X4, 6, BANK), list3, list4, SUB),
+            (score(shelves, shelves_plane, 4, FP8X4, 0, BANK), list5, list6, ADD),
+        ]
+        for s, (banks, take, put, op) in enumerate(stages):
+            picked = look_up(table, take, "picked%d" % s)
+            nc.vector.tensor_copy(placed[s][:].indirect(put[:]), picked[:])
+            table = held.tile([P, POOL], F32, name="table%d" % s)
+            for piece, bank in enumerate(banks):
+                cols = slice(piece * BANK, (piece + 1) * BANK)
+                nc.vector.tensor_tensor(table[:, cols], bank[:], placed[s][:, cols], op)
+
+        result = look_up(table, list7, "result")
+        nc.sync.dma_start(out[:, :HALF], result[:, :HALF])
+        nc.scalar.dma_start(out[:, HALF:], result[:, HALF:])

@@ -52,8 +52,8 @@ def tile_attend_relayfour_four_kernel(
 
         q_raw = held.tile([P, PACK, Q], F32, name="q_raw")
         nc.sync.dma_start(q_raw[:], query.rearrange("(p j) q -> p j q", j=PACK))
-        keys_plane = load_scales(keys_scales, "keys_plane", nc.scalar)
         keys = load_words(keys_words[0], "keys", 2)
+        keys_plane = load_scales(keys_scales, "keys_plane", nc.sync)
         list1 = load_list(offs, "list1")
         list2 = load_list(offs2, "list2")
         notes_plane = load_scales(notes_scales, "notes_plane", nc.sync)
@@ -68,23 +68,27 @@ def tile_attend_relayfour_four_kernel(
         shelves = load_words(shelves_words[0].rearrange("p n t -> p (n t)"), "shelves", 4)
         list7 = load_list(offs7, "list7")
 
-        placed = [held.tile([P, POOL], F32, name="placed%d" % s) for s in range(3)]
-        for tile in placed:
-            nc.vector.memset(tile[:], 0.0)
+        placed = [held.tile([P, POOL], F32, name="placed%d" % s) for s in range(2)]
+        nc.vector.memset(placed[0][:], 0.0)
+        nc.gpsimd.memset(placed[1][:], 0.0)
 
-        q_bf = held.tile([P, Q, PACK], BF16, name="q_bf", align_bytes=64)
+        q_bf = held.tile([P, Q, PACK], BF16, name="q_bf", tag="reused", align_bytes=64)
         nc.vector.tensor_copy(q_bf[:], q_raw[:].rearrange("p j q -> p q j"))
         q_codes = held.tile([P, Q], U32, name="q_codes", align_bytes=64)
         q_plane = held.tile([P, Q], U8, name="q_plane", align_bytes=64)
         nc.vector.quantize_mx(
             out=q_codes[:].bitcast(FP8X4), scales=q_plane[:], in_=q_bf[:].rearrange("p q j -> p (q j)")
         )
+        last = held.tile([P, POOL], F32, name="placed2", tag="reused", align_bytes=64)
+        nc.gpsimd.memset(last[:], 0.0)
+        placed.append(last)
 
-        def score(words, plane, width, dtype, first_bank, cols):
+        def score(words, plane, width, dtype, first_bank, pieces):
             banks = []
-            for piece in range(POOL // cols):
-                bank = psum.tile([P, cols], F32, name="bank%d" % (first_bank + piece))
-                lo, hi = piece * cols, (piece + 1) * cols
+            hi = 0
+            for piece, cols in enumerate(pieces):
+                bank = psum.tile([P, cols], F32, name="bank%d" % ((first_bank + piece) % 8))
+                lo, hi = hi, hi + cols
                 nc.tensor.matmul_mx(
                     bank[:],
                     lhsT=q_codes[:].bitcast(FP8X4),
@@ -103,28 +107,31 @@ def tile_attend_relayfour_four_kernel(
             nc.scalar.activation(picked[:, HALF:], table[:].indirect(offsets[:, LIST_COLS // 2 :]), COPY)
             return picked
 
-        A_COLS = 256
-        a_banks = score(keys, keys_plane, 2, FP4X4, 0, A_COLS)
-        table = held.tile([P, POOL], F32, name="a")
+        a_pieces = [256,256,256,128,128]
+        a_banks = score(keys, keys_plane, 2, FP4X4, 0, a_pieces)
+        table = held.tile([P, POOL], F32, name="table")
+        hi = 0
         for piece, bank in enumerate(a_banks):
-            cols = table[:, piece * A_COLS : (piece + 1) * A_COLS]
+            lo, hi = hi, hi + a_pieces[piece]
             if piece % 2 == 0:
-                nc.scalar.activation(cols, bank[:], COPY)
+                nc.scalar.activation(table[:, lo:hi], bank[:], COPY)
             else:
-                nc.vector.tensor_copy(cols, bank[:])
+                nc.vector.tensor_copy(table[:, lo:hi], bank[:])
 
         stages = [
-            (score(notes, notes_plane, 4, FP8X4, 4, BANK), list1, list2, ADD),
-            (score(users, users_plane, 2, FP4X4, 6, BANK), list3, list4, SUB),
-            (score(shelves, shelves_plane, 4, FP8X4, 0, BANK), list5, list6, ADD),
+            (score(notes, notes_plane, 4, FP8X4, 5, [BANK, BANK]), list1, list2, ADD),
+            (score(users, users_plane, 2, FP4X4, 7, [BANK, BANK]), list3, list4, SUB),
+            (score(shelves, shelves_plane, 4, FP8X4, 1, [BANK, BANK]), list5, list6, ADD),
         ]
+        split = POOL - 320
         for s, (banks, take, put, op) in enumerate(stages):
             picked = look_up(table, take, "picked%d" % s)
             nc.vector.tensor_copy(placed[s][:].indirect(put[:]), picked[:])
-            table = held.tile([P, POOL], F32, name="table%d" % s)
-            for piece, bank in enumerate(banks):
-                cols = slice(piece * BANK, (piece + 1) * BANK)
-                nc.vector.tensor_tensor(table[:, cols], bank[:], placed[s][:, cols], op)
+            table = held.tile([P, POOL], F32, name="table")
+            nc.scalar.activation(table[:, split:], banks[1][:, split - BANK :], COPY)
+            nc.gpsimd.tensor_tensor(table[:, split:], table[:, split:], placed[s][:, split:], op)
+            nc.vector.tensor_tensor(table[:, :BANK], banks[0][:], placed[s][:, :BANK], op)
+            nc.vector.tensor_tensor(table[:, BANK:split], banks[1][:, : split - BANK], placed[s][:, BANK:split], op)
 
         result = look_up(table, list7, "result")
         nc.sync.dma_start(out[:, :HALF], result[:, :HALF])

@@ -52,8 +52,10 @@ def tile_attend_relayfour_four_kernel(
 
         q_raw = held.tile([P, PACK, Q], F32, name="q_raw")
         nc.sync.dma_start(q_raw[:], query.rearrange("(p j) q -> p j q", j=PACK))
-        keys = load_words(keys_words[0], "keys", 2)
+        keys = held.tile([P, POOL * 2], U8, name="keys", align_bytes=64)
+        nc.sync.dma_start(keys[:, :POOL].bitcast(I32), keys_words[0][:, :POOL].bitcast(I32))
         keys_plane = load_scales(keys_scales, "keys_plane", nc.sync)
+        nc.sync.dma_start(keys[:, POOL:].bitcast(I32), keys_words[0][:, POOL:].bitcast(I32))
         list1 = load_list(offs, "list1")
         list2 = load_list(offs2, "list2")
         notes_plane = load_scales(notes_scales, "notes_plane", nc.sync)
@@ -73,7 +75,9 @@ def tile_attend_relayfour_four_kernel(
         nc.gpsimd.memset(placed[1][:], 0.0)
 
         q_bf = held.tile([P, Q, PACK], BF16, name="q_bf", tag="reused", align_bytes=64)
-        nc.vector.tensor_copy(q_bf[:], q_raw[:].rearrange("p j q -> p q j"))
+        nc.vector.tensor_copy(
+            q_bf[:].rearrange("p (c i) j -> p c j i", i=4), q_raw[:].rearrange("p j (c i) -> p c j i", i=4)
+        )
         q_codes = held.tile([P, Q], U32, name="q_codes", align_bytes=64)
         q_plane = held.tile([P, Q], U8, name="q_plane", align_bytes=64)
         nc.vector.quantize_mx(
@@ -123,7 +127,7 @@ def tile_attend_relayfour_four_kernel(
             (score(users, users_plane, 2, FP4X4, 7, [BANK, BANK]), list3, list4, SUB),
             (score(shelves, shelves_plane, 4, FP8X4, 1, [BANK, BANK]), list5, list6, ADD),
         ]
-        split = POOL - 320
+        split = POOL - 256
         for s, (banks, take, put, op) in enumerate(stages):
             picked = look_up(table, take, "picked%d" % s)
             nc.vector.tensor_copy(placed[s][:].indirect(put[:]), picked[:])

@@ -52,9 +52,9 @@ def tile_attend_relayfour_four_kernel(
 
         q_raw = held.tile([P, PACK, Q], F32, name="q_raw")
         nc.sync.dma_start(q_raw[:], query.rearrange("(p j) q -> p j q", j=PACK))
+        keys_plane = load_scales(keys_scales, "keys_plane", nc.sync)
         keys = held.tile([P, POOL * 2], U8, name="keys", align_bytes=64)
         nc.sync.dma_start(keys[:, :POOL].bitcast(I32), keys_words[0][:, :POOL].bitcast(I32))
-        keys_plane = load_scales(keys_scales, "keys_plane", nc.sync)
         nc.sync.dma_start(keys[:, POOL:].bitcast(I32), keys_words[0][:, POOL:].bitcast(I32))
         list1 = load_list(offs, "list1")
         list2 = load_list(offs2, "list2")

@@ -19,9 +19,13 @@ COPY = mybir.ActivationFunctionType.Copy
 
 P = 128
 PACK = 4
+FP8_BYTES, FP4_BYTES = 4, 2
 BANK = 512
-HALF = SLOTS // 2
+BANKS = 8
 LIST_COLS = SLOTS // 16
+
+A_PIECES = [256, 256, 256, 128, 128]
+GPSIMD_COLS = 288
 
 
 def tile_attend_relayfour_four_kernel(
@@ -38,66 +42,76 @@ def tile_attend_relayfour_four_kernel(
             nc.sync.dma_start(tile[:], source)
             return tile
 
-        def load_scales(source, name, queue):
+        def load_scales(source, name):
             plane = held.tile([P, POOL], U8, name=name, align_bytes=64)
             rows = source[0].bitcast(I32)
             for quad in range(4):
-                queue.dma_start(plane[32 * quad : 32 * quad + 4, :].bitcast(I32), rows[4 * quad : 4 * quad + 4, :])
+                nc.sync.dma_start(
+                    plane[32 * quad : 32 * quad + 4, :].bitcast(I32), rows[4 * quad : 4 * quad + 4, :]
+                )
             return plane
 
-        def load_words(source, name, width):
-            words = held.tile([P, POOL * width], U8, name=name, align_bytes=64)
+        def load_words(source, name, word_bytes):
+            words = held.tile([P, POOL * word_bytes], U8, name=name, align_bytes=64)
             nc.sync.dma_start(words[:].bitcast(I32), source.bitcast(I32))
             return words
 
         q_raw = held.tile([P, PACK, Q], F32, name="q_raw")
         nc.sync.dma_start(q_raw[:], query.rearrange("(p j) q -> p j q", j=PACK))
-        keys_plane = load_scales(keys_scales, "keys_plane", nc.sync)
-        keys = held.tile([P, POOL * 2], U8, name="keys", align_bytes=64)
-        nc.sync.dma_start(keys[:, :POOL].bitcast(I32), keys_words[0][:, :POOL].bitcast(I32))
-        nc.sync.dma_start(keys[:, POOL:].bitcast(I32), keys_words[0][:, POOL:].bitcast(I32))
+        keys = held.tile([P, POOL * FP4_BYTES], U8, name="keys", align_bytes=64)
+        half_bytes = POOL * FP4_BYTES // 2
+        nc.sync.dma_start(keys[:, :half_bytes].bitcast(I32), keys_words[0][:, :half_bytes].bitcast(I32))
+        keys_plane = load_scales(keys_scales, "keys_plane")
+        nc.sync.dma_start(keys[:, half_bytes:].bitcast(I32), keys_words[0][:, half_bytes:].bitcast(I32))
         list1 = load_list(offs, "list1")
         list2 = load_list(offs2, "list2")
-        notes_plane = load_scales(notes_scales, "notes_plane", nc.sync)
-        notes = load_words(notes_words[0].rearrange("p n t -> p (n t)"), "notes", 4)
+        notes_plane = load_scales(notes_scales, "notes_plane")
+        notes = load_words(notes_words[0].rearrange("p n t -> p (n t)"), "notes", FP8_BYTES)
         list3 = load_list(offs3, "list3")
         list4 = load_list(offs4, "list4")
-        users_plane = load_scales(users_scales, "users_plane", nc.sync)
-        users = load_words(users_words[0], "users", 2)
+        users_plane = load_scales(users_scales, "users_plane")
+        users = load_words(users_words[0], "users", FP4_BYTES)
         list5 = load_list(offs5, "list5")
         list6 = load_list(offs6, "list6")
-        shelves_plane = load_scales(shelves_scales, "shelves_plane", nc.sync)
-        shelves = load_words(shelves_words[0].rearrange("p n t -> p (n t)"), "shelves", 4)
+        shelves_plane = load_scales(shelves_scales, "shelves_plane")
+        shelves = load_words(shelves_words[0].rearrange("p n t -> p (n t)"), "shelves", FP8_BYTES)
         list7 = load_list(offs7, "list7")
 
-        placed = [held.tile([P, POOL], F32, name="placed%d" % s) for s in range(2)]
-        nc.vector.memset(placed[0][:], 0.0)
-        nc.gpsimd.memset(placed[1][:], 0.0)
+        windows = [held.tile([P, POOL], F32, name="window%d" % s) for s in range(2)]
+        nc.vector.memset(windows[0][:], 0.0)
+        nc.gpsimd.memset(windows[1][:], 0.0)
 
-        q_bf = held.tile([P, Q, PACK], BF16, name="q_bf", tag="reused", align_bytes=64)
-        nc.vector.tensor_copy(
-            q_bf[:].rearrange("p (c i) j -> p c j i", i=4), q_raw[:].rearrange("p j (c i) -> p c j i", i=4)
-        )
+        q_bf = held.tile([P, Q, PACK], BF16, name="q_bf", tag="q_bf_then_window", align_bytes=64)
         q_codes = held.tile([P, Q], U32, name="q_codes", align_bytes=64)
         q_plane = held.tile([P, Q], U8, name="q_plane", align_bytes=64)
-        nc.vector.quantize_mx(
-            out=q_codes[:].bitcast(FP8X4), scales=q_plane[:], in_=q_bf[:].rearrange("p q j -> p (q j)")
-        )
-        last = held.tile([P, POOL], F32, name="placed2", tag="reused", align_bytes=64)
-        nc.gpsimd.memset(last[:], 0.0)
-        placed.append(last)
+        row_halves = [slice(0, Q // 2), slice(Q // 2, Q)]
+        for rows in row_halves:
+            nc.vector.tensor_copy(
+                q_bf[:, rows, :].rearrange("p (c i) j -> p c j i", i=4),
+                q_raw[:, :, rows].rearrange("p j (c i) -> p c j i", i=4),
+            )
+        for rows in row_halves:
+            nc.vector.quantize_mx(
+                out=q_codes[:, rows].bitcast(FP8X4),
+                scales=q_plane[:, rows],
+                in_=q_bf[:, rows, :].rearrange("p q j -> p (q j)"),
+            )
 
-        def score(words, plane, width, dtype, first_bank, pieces):
+        last_window = held.tile([P, POOL], F32, name="window2", tag="q_bf_then_window", align_bytes=64)
+        nc.gpsimd.memset(last_window[:], 0.0)
+        windows.append(last_window)
+
+        def score(words, plane, word_bytes, dtype, first_bank, pieces):
             banks = []
             hi = 0
-            for piece, cols in enumerate(pieces):
-                bank = psum.tile([P, cols], F32, name="bank%d" % ((first_bank + piece) % 8))
-                lo, hi = hi, hi + cols
+            for piece, width in enumerate(pieces):
+                bank = psum.tile([P, width], F32, name="bank%d" % ((first_bank + piece) % BANKS))
+                lo, hi = hi, hi + width
                 nc.tensor.matmul_mx(
                     bank[:],
                     lhsT=q_codes[:].bitcast(FP8X4),
                     lhsT_scale=q_plane[:],
-                    rhs=words[:, lo * width : hi * width].bitcast(dtype),
+                    rhs=words[:, lo * word_bytes : hi * word_bytes].bitcast(dtype),
                     rhs_scale=plane[:, lo:hi],
                     start=True,
                     stop=True,
@@ -107,36 +121,38 @@ def tile_attend_relayfour_four_kernel(
 
         def look_up(table, offsets, name):
             picked = held.tile([P, SLOTS], F32, name=name)
-            nc.vector.tensor_copy(picked[:, :HALF], table[:].indirect(offsets[:, : LIST_COLS // 2]))
-            nc.scalar.activation(picked[:, HALF:], table[:].indirect(offsets[:, LIST_COLS // 2 :]), COPY)
+            nc.vector.tensor_copy(picked[:, : SLOTS // 2], table[:].indirect(offsets[:, : LIST_COLS // 2]))
+            nc.scalar.activation(picked[:, SLOTS // 2 :], table[:].indirect(offsets[:, LIST_COLS // 2 :]), COPY)
             return picked
 
-        a_pieces = [256,256,256,128,128]
-        a_banks = score(keys, keys_plane, 2, FP4X4, 0, a_pieces)
+        a_banks = score(keys, keys_plane, FP4_BYTES, FP4X4, 0, A_PIECES)
         table = held.tile([P, POOL], F32, name="table")
         hi = 0
         for piece, bank in enumerate(a_banks):
-            lo, hi = hi, hi + a_pieces[piece]
+            lo, hi = hi, hi + A_PIECES[piece]
             if piece % 2 == 0:
                 nc.scalar.activation(table[:, lo:hi], bank[:], COPY)
             else:
                 nc.vector.tensor_copy(table[:, lo:hi], bank[:])
 
+        two_banks = [BANK, BANK]
+        b_bank = len(A_PIECES)
         stages = [
-            (score(notes, notes_plane, 4, FP8X4, 5, [BANK, BANK]), list1, list2, ADD),
-            (score(users, users_plane, 2, FP4X4, 7, [BANK, BANK]), list3, list4, SUB),
-            (score(shelves, shelves_plane, 4, FP8X4, 1, [BANK, BANK]), list5, list6, ADD),
+            (score(notes, notes_plane, FP8_BYTES, FP8X4, b_bank, two_banks), list1, list2, ADD),
+            (score(users, users_plane, FP4_BYTES, FP4X4, b_bank + 2, two_banks), list3, list4, SUB),
+            (score(shelves, shelves_plane, FP8_BYTES, FP8X4, b_bank + 4, two_banks), list5, list6, ADD),
         ]
-        split = POOL - 256
+        split = POOL - GPSIMD_COLS
         for s, (banks, take, put, op) in enumerate(stages):
+            window = windows[s]
             picked = look_up(table, take, "picked%d" % s)
-            nc.vector.tensor_copy(placed[s][:].indirect(put[:]), picked[:])
+            nc.vector.tensor_copy(window[:].indirect(put[:]), picked[:])
             table = held.tile([P, POOL], F32, name="table")
             nc.scalar.activation(table[:, split:], banks[1][:, split - BANK :], COPY)
-            nc.gpsimd.tensor_tensor(table[:, split:], table[:, split:], placed[s][:, split:], op)
-            nc.vector.tensor_tensor(table[:, :BANK], banks[0][:], placed[s][:, :BANK], op)
-            nc.vector.tensor_tensor(table[:, BANK:split], banks[1][:, : split - BANK], placed[s][:, BANK:split], op)
+            nc.gpsimd.tensor_tensor(table[:, split:], table[:, split:], window[:, split:], op)
+            nc.vector.tensor_tensor(table[:, :BANK], banks[0][:], window[:, :BANK], op)
+            nc.vector.tensor_tensor(table[:, BANK:split], banks[1][:, : split - BANK], window[:, BANK:split], op)
 
         result = look_up(table, list7, "result")
-        nc.sync.dma_start(out[:, :HALF], result[:, :HALF])
-        nc.scalar.dma_start(out[:, HALF:], result[:, HALF:])
+        nc.sync.dma_start(out[:, : SLOTS // 2], result[:, : SLOTS // 2])
+        nc.scalar.dma_start(out[:, SLOTS // 2 :], result[:, SLOTS // 2 :])

from contextlib import ExitStack

import concourse.mybir as mybir

D, POOL, SLOTS, Q = 512, 1024, 512, 128
FLOPS = 4 * 2 * D * POOL * Q

F32 = mybir.dt.float32
BF16 = mybir.dt.bfloat16
I32 = mybir.dt.int32
U32 = mybir.dt.uint32
U16 = mybir.dt.uint16
U8 = mybir.dt.uint8
FP8X4 = mybir.dt.float8_e4m3fn_x4
FP4X4 = mybir.dt.float4_e2m1fn_x4
ADD = mybir.AluOpType.add
SUB = mybir.AluOpType.subtract
COPY = mybir.ActivationFunctionType.Copy

P = 128
PACK = 4
FP8_BYTES, FP4_BYTES = 4, 2
BANK = 512
BANKS = 8
LIST_COLS = SLOTS // 16

A_PIECES = [256, 256, 256, 128, 128]
GPSIMD_COLS = 288


def tile_attend_relayfour_four_kernel(
    tc, query, keys_words, keys_scales, notes_words, notes_scales, users_words, users_scales,
    shelves_words, shelves_scales, offs, offs2, offs3, offs4, offs5, offs6, offs7, out,
):
    nc = tc.nc
    with ExitStack() as ctx:
        held = ctx.enter_context(tc.tile_pool(name="held", bufs=1))
        psum = ctx.enter_context(tc.psum_pool(name="psum", bufs=1))

        def load_list(source, name):
            tile = held.tile([P, LIST_COLS], U16, name=name)
            nc.sync.dma_start(tile[:], source)
            return tile

        def load_scales(source, name):
            plane = held.tile([P, POOL], U8, name=name, align_bytes=64)
            rows = source[0].bitcast(I32)
            for quad in range(4):
                nc.sync.dma_start(
                    plane[32 * quad : 32 * quad + 4, :].bitcast(I32), rows[4 * quad : 4 * quad + 4, :]
                )
            return plane

        def load_words(source, name, word_bytes):
            words = held.tile([P, POOL * word_bytes], U8, name=name, align_bytes=64)
            nc.sync.dma_start(words[:].bitcast(I32), source.bitcast(I32))
            return words

        q_raw = held.tile([P, PACK, Q], F32, name="q_raw")
        nc.sync.dma_start(q_raw[:], query.rearrange("(p j) q -> p j q", j=PACK))
        keys = held.tile([P, POOL * FP4_BYTES], U8, name="keys", align_bytes=64)
        half_bytes = POOL * FP4_BYTES // 2
        nc.sync.dma_start(keys[:, :half_bytes].bitcast(I32), keys_words[0][:, :half_bytes].bitcast(I32))
        keys_plane = load_scales(keys_scales, "keys_plane")
        nc.sync.dma_start(keys[:, half_bytes:].bitcast(I32), keys_words[0][:, half_bytes:].bitcast(I32))
        list1 = load_list(offs, "list1")
        list2 = load_list(offs2, "list2")
        notes_plane = load_scales(notes_scales, "notes_plane")
        notes = load_words(notes_words[0].rearrange("p n t -> p (n t)"), "notes", FP8_BYTES)
        list3 = load_list(offs3, "list3")
        list4 = load_list(offs4, "list4")
        users_plane = load_scales(users_scales, "users_plane")
        users = load_words(users_words[0], "users", FP4_BYTES)
        list5 = load_list(offs5, "list5")
        list6 = load_list(offs6, "list6")
        shelves_plane = load_scales(shelves_scales, "shelves_plane")
        shelves = load_words(shelves_words[0].rearrange("p n t -> p (n t)"), "shelves", FP8_BYTES)
        list7 = load_list(offs7, "list7")

        windows = [held.tile([P, POOL], F32, name="window%d" % s) for s in range(2)]
        nc.vector.memset(windows[0][:], 0.0)
        nc.gpsimd.memset(windows[1][:], 0.0)

        q_bf = held.tile([P, Q, PACK], BF16, name="q_bf", tag="q_bf_then_window", align_bytes=64)
        q_codes = held.tile([P, Q], U32, name="q_codes", align_bytes=64)
        q_plane = held.tile([P, Q], U8, name="q_plane", align_bytes=64)
        row_halves = [slice(0, Q // 2), slice(Q // 2, Q)]
        for rows in row_halves:
            nc.vector.tensor_copy(
                q_bf[:, rows, :].rearrange("p (c i) j -> p c j i", i=4),
                q_raw[:, :, rows].rearrange("p j (c i) -> p c j i", i=4),
            )
        for rows in row_halves:
            nc.vector.quantize_mx(
                out=q_codes[:, rows].bitcast(FP8X4),
                scales=q_plane[:, rows],
                in_=q_bf[:, rows, :].rearrange("p q j -> p (q j)"),
            )

        last_window = held.tile([P, POOL], F32, name="window2", tag="q_bf_then_window", align_bytes=64)
        nc.gpsimd.memset(last_window[:], 0.0)
        windows.append(last_window)

        def score(words, plane, word_bytes, dtype, first_bank, pieces):
            banks = []
            hi = 0
            for piece, width in enumerate(pieces):
                bank = psum.tile([P, width], F32, name="bank%d" % ((first_bank + piece) % BANKS))
                lo, hi = hi, hi + width
                nc.tensor.matmul_mx(
                    bank[:],
                    lhsT=q_codes[:].bitcast(FP8X4),
                    lhsT_scale=q_plane[:],
                    rhs=words[:, lo * word_bytes : hi * word_bytes].bitcast(dtype),
                    rhs_scale=plane[:, lo:hi],
                    start=True,
                    stop=True,
                )
                banks.append(bank)
            return banks

        def look_up(table, offsets, name):
            picked = held.tile([P, SLOTS], F32, name=name)
            nc.vector.tensor_copy(picked[:, : SLOTS // 2], table[:].indirect(offsets[:, : LIST_COLS // 2]))
            nc.scalar.activation(picked[:, SLOTS // 2 :], table[:].indirect(offsets[:, LIST_COLS // 2 :]), COPY)
            return picked

        a_banks = score(keys, keys_plane, FP4_BYTES, FP4X4, 0, A_PIECES)
        table = held.tile([P, POOL], F32, name="table")
        hi = 0
        for piece, bank in enumerate(a_banks):
            lo, hi = hi, hi + A_PIECES[piece]
            if piece % 2 == 0:
                nc.scalar.activation(table[:, lo:hi], bank[:], COPY)
            else:
                nc.vector.tensor_copy(table[:, lo:hi], bank[:])

        two_banks = [BANK, BANK]
        b_bank = len(A_PIECES)
        stages = [
            (score(notes, notes_plane, FP8_BYTES, FP8X4, b_bank, two_banks), list1, list2, ADD),
            (score(users, users_plane, FP4_BYTES, FP4X4, b_bank + 2, two_banks), list3, list4, SUB),
            (score(shelves, shelves_plane, FP8_BYTES, FP8X4, b_bank + 4, two_banks), list5, list6, ADD),
        ]
        split = POOL - GPSIMD_COLS
        for s, (banks, take, put, op) in enumerate(stages):
            window = windows[s]
            picked = look_up(table, take, "picked%d" % s)
            nc.vector.tensor_copy(window[:].indirect(put[:]), picked[:])
            table = held.tile([P, POOL], F32, name="table")
            nc.scalar.activation(table[:, split:], banks[1][:, split - BANK :], COPY)
            nc.gpsimd.tensor_tensor(table[:, split:], table[:, split:], window[:, split:], op)
            nc.vector.tensor_tensor(table[:, :BANK], banks[0][:], window[:, :BANK], op)
            nc.vector.tensor_tensor(table[:, BANK:split], banks[1][:, : split - BANK], window[:, BANK:split], op)

        result = look_up(table, list7, "result")
        nc.sync.dma_start(out[:, : SLOTS // 2], result[:, : SLOTS // 2])
        nc.scalar.dma_start(out[:, SLOTS // 2 :], result[:, SLOTS // 2 :])
